import numpy as np
import ml_dtypes


def mxq(x, axis, fmt="e4m3"):
    dtype, down = {"e4m3": (ml_dtypes.float8_e4m3fn, 7), "e5m2": (ml_dtypes.float8_e5m2, 14)}[fmt]
    v = np.moveaxis(np.asarray(x, np.float32).astype(ml_dtypes.bfloat16).astype(np.float64), axis, -1)
    blocks = v.reshape(v.shape[:-1] + (-1, 32))
    amax = np.abs(blocks).max(-1, keepdims=True)
    byte = np.maximum(np.where(amax > 0, np.frexp(amax)[1] - 1 + 127, 0) - down, 1)
    scale = np.exp2(byte - 127.0)
    codes = (blocks / scale).astype(np.float32).astype(dtype).astype(np.float64)
    return np.moveaxis((codes * scale).reshape(v.shape), -1, axis)


WIDE = False


def mx_kscale(k):
    if not WIDE:
        return np.ones(k)
    levels = np.array([10, -10, 5, -5, 0])
    if k % 512:
        return np.exp2(np.random.permutation(np.resize(levels, k // 32))).repeat(32)
    a = np.empty((k // 512, 16))
    for p in range(k // 512):
        a[p, :8] = np.random.permutation(np.resize(levels, 8))
        for g in range(8):
            far = levels[np.abs(levels - a[p, g]) >= 10]
            a[p, g + 8] = far[np.random.randint(len(far))]
    return np.exp2(a.ravel()).repeat(32)


def f64(x):
    return np.asarray(x).astype(np.float64)


def striped(idx):
    return np.tile(idx.reshape(-1, 16).T, (8, 1)).astype(np.uint16)


def unstriped(offs):
    return offs[:16].T.reshape(-1).astype(np.int64)


def striped8(idx):
    return np.concatenate([x.reshape(-1, 16).T for x in idx]).astype(np.uint16)


def runs(offs, k):
    lists = np.stack([offs[16 * r : 16 * r + 16].T.reshape(-1) for r in range(8)]).astype(np.int64)
    return lists[np.arange(k) % 512 // 64]


def pack_weight(w):
    k, n = w.shape
    w = f64(np.asarray(w, np.float32).astype(ml_dtypes.bfloat16)).reshape(k // 32, 32, n)
    amax = np.abs(w).max(1)
    byte = np.clip(np.where(amax > 0, np.frexp(amax)[1] - 1 + 127 - 7, 1), 1, 254)
    scaled = (w * np.exp2(127.0 - byte)[:, None, :]).reshape(k, n).astype(np.float32)
    words = np.ascontiguousarray(scaled.reshape(k // 512, 128, 4, n).transpose(0, 1, 3, 2)).astype(ml_dtypes.float8_e4m3fn).view(np.uint8)
    return words, np.ascontiguousarray(byte.astype(np.uint8).reshape(k // 512, 16, n))


def unpack_weight(words, scales):
    g, p, n, _ = words.shape
    vals = np.ascontiguousarray(words).view(ml_dtypes.float8_e4m3fn).astype(np.float64) * np.repeat(np.exp2(scales.astype(np.float64) - 127.0), 8, axis=1)[..., None]
    return vals.transpose(0, 1, 3, 2).reshape(g * 512, n)


E2M1 = np.array([0.0, 0.5, 1.0, 1.5, 2.0, 3.0, 4.0, 6.0, -0.0, -0.5, -1.0, -1.5, -2.0, -3.0, -4.0, -6.0])


def pack_fp4(w):
    k, n = w.shape
    w = f64(np.asarray(w, np.float32).astype(ml_dtypes.bfloat16)).reshape(k // 32, 32, n)
    amax = np.abs(w).max(1)
    mant, ex = np.frexp(amax / 6.0)
    byte = np.clip(np.where(amax > 0, np.where(mant > 0.5, ex, ex - 1) + 127, 1), 1, 254)
    scaled = (w * np.exp2(127.0 - byte)[:, None, :]).reshape(k, n).astype(np.float32)
    c = np.ascontiguousarray(scaled.reshape(k // 512, 128, 4, n).transpose(0, 1, 3, 2)).astype(ml_dtypes.float4_e2m1fn).view(np.uint8) & 0xF
    words = (c[..., 0::2] | (c[..., 1::2] << 4)).reshape(k // 512, 128, 2 * n)
    return np.ascontiguousarray(words), np.ascontiguousarray(byte.astype(np.uint8).reshape(k // 512, 16, n))


def unpack_fp4(words, scales):
    g, _, n = scales.shape
    words = np.ascontiguousarray(words).reshape(g, 128, n, 2)
    nib = np.empty((g, 128, n, 4), np.uint8)
    nib[..., 0::2] = words & 0xF
    nib[..., 1::2] = words >> 4
    vals = E2M1[nib] * np.repeat(np.exp2(scales.astype(np.float64) - 127.0), 8, axis=1)[..., None]
    return vals.transpose(0, 1, 3, 2).reshape(g * 512, n)


def planes(y):
    n, m = y.shape
    v = y.astype(np.float32).astype(ml_dtypes.bfloat16).astype(np.float64).reshape(n // 32, 32, m)
    top = np.abs(v).max(1)
    byte = np.clip(np.where(top > 0, np.frexp(top)[1] - 1 + 127 - 7, 1), 1, 254)
    codes = (v * np.exp2(127.0 - byte)[:, None, :]).reshape(n, m).astype(np.float32).astype(ml_dtypes.float8_e4m3fn).view(np.uint8)
    words = codes.reshape(n // 512, 128, 4, m).transpose(0, 1, 3, 2)
    return np.ascontiguousarray(words), np.ascontiguousarray(byte.astype(np.uint8).reshape(n // 512, 16, m))


K, T, S, V, N, H = 512, 2048, 512, 256, 512, 512


def setup_inputs():
    n = np.random.standard_normal
    s = mx_kscale(K)[:, None]
    u = mx_kscale(H)
    packed_xT = pack_weight(n((K, T)) * s)
    packed_w1 = pack_fp4(n((K, H)) / np.sqrt(K) / s)
    packed_w2 = pack_fp4(n((H, N)) / np.sqrt(H) / u[:, None])
    return {
        "x_words": packed_xT[0],
        "x_scales": packed_xT[1],
        "w1_words": packed_w1[0],
        "w1_scales": packed_w1[1],
        "dep": np.repeat(np.random.uniform(0.5, 2.0, (8, V)), 64, axis=0).astype(np.float32),
        "gn": (np.random.uniform(0.5, 1.5, (H, 1)) * u[:, None]).astype(np.float32),
        "w2_words": packed_w2[0],
        "w2_scales": packed_w2[1],
        "res": (2 * n((N, V))).astype(np.float32),
        "offs": striped(np.random.permutation(T)[:S]),
        "i_l": striped8(np.stack([np.random.permutation(S)[:V] for _ in range(8)])),
        "j_l": striped8(np.stack([np.random.permutation(S)[:V] for _ in range(8)])),
    }


def reference(x_words, x_scales, w1_words, w1_scales, dep, gn, w2_words, w2_scales, res, offs, i_l, j_l):
    xq = unpack_weight(x_words, x_scales)[:, unstriped(offs)]
    y = unpack_fp4(w1_words, w1_scales).T @ xq
    mo = -1.0 * (np.exp(-1.0 * (np.abs(y[np.arange(H)[:, None], runs(i_l, H)] - (y[np.arange(H)[:, None], runs(j_l, H)]))))) + 1
    z = f64(gn) * (f64(dep) * ((mo) ** 2))
    out_0 = f64(res) + (unpack_fp4(w2_words, w2_scales).T @ mxq(z, 0, "e4m3"))
    return (out_0,) + planes(out_0)

@@ -1,0 +1,186 @@
+from contextlib import ExitStack
+
+import concourse.mybir as mybir
+
+F32 = mybir.dt.float32
+BF16 = mybir.dt.bfloat16
+I32 = mybir.dt.int32
+U32 = mybir.dt.uint32
+U16 = mybir.dt.uint16
+U8 = mybir.dt.uint8
+FP8X4 = mybir.dt.float8_e4m3fn_x4
+FP4X4 = mybir.dt.float4_e2m1fn_x4
+ACT = mybir.ActivationFunctionType
+ALU = mybir.AluOpType
+
+P = 128
+PACK = 4
+K, T, S, V, H, N = 512, 2048, 512, 256, 512, 512
+SH = S // 2
+VH = V // 2
+FLOPS = 2 * K * H * S + 2 * H * N * V
+
+
+def load_scale_rows(queues, plane, rows):
+    for q in range(4):
+        queues[q].dma_start(out=plane[32 * q : 32 * q + 4, :].bitcast(I32), in_=rows[4 * q : 4 * q + 4, :].bitcast(I32))
+
+
+def deal_words(nc, dealt, raw):
+    nc.vector.tensor_copy(
+        out=dealt[:].rearrange("p t (m b) -> p t m b", b=2),
+        in_=raw[:].rearrange("p (m t b) -> p t m b", t=PACK, b=2),
+    )
+
+
+def deal_scales(nc, dealt, raw):
+    nc.vector.tensor_copy(out=dealt[:], in_=raw[:].rearrange("p (m t) -> p t m", t=PACK))
+
+
+def tile_picked_morse8_none_po_kernel(
+    tc, x_words, x_scales, w1_words, w1_scales, dep, gn, w2_words, w2_scales, res, offs, i_l, j_l, out_0, out_1, out_2
+):
+    nc = tc.nc
+    with ExitStack() as ctx:
+        lists = ctx.enter_context(tc.tile_pool(name="lists", bufs=1))
+        sb = ctx.enter_context(tc.tile_pool(name="sb", bufs=1))
+        ps = ctx.enter_context(tc.psum_pool(name="ps", bufs=1))
+
+        offs_t = lists.tile([P, S // 16], U16, name="offs_t")
+        i_t = lists.tile([P, V // 16], U16, name="i_t")
+        j_t = lists.tile([P, V // 16], U16, name="j_t")
+
+        xs_raw = sb.tile([P, T], U8, name="xs_raw")
+        w1s_raw = sb.tile([P, H], U8, name="w1s_raw", tag="w1s_xq", align_bytes=64)
+        w2s_raw = sb.tile([P, N], U8, name="w2s_raw")
+        zero = sb.tile([P, 1], F32, name="zero")
+        nc.vector.memset(xs_raw[:].bitcast(I32), 0)
+        nc.gpsimd.memset(w1s_raw[:].bitcast(I32), 0)
+        nc.vector.memset(w2s_raw[:].bitcast(I32), 0)
+        nc.vector.memset(zero[:], 0.0)
+
+        xw = sb.tile([P, T], U32, name="xw", tag="xw_w2d", align_bytes=64)
+        w_raw = sb.tile([P, 2 * H], U8, name="w_raw")
+        nc.sync.dma_start(offs_t[:], offs)
+        nc.sync.dma_start(out=w_raw[:].bitcast(I32), in_=w1_words[0].bitcast(I32))
+        nc.sync.dma_start(out=xw[:].bitcast(I32), in_=x_words[0].rearrange("p n t -> p (n t)").bitcast(I32))
+        load_scale_rows([nc.scalar] * 4, xs_raw, x_scales[0])
+        load_scale_rows([nc.scalar] * 3 + [nc.gpsimd], w1s_raw, w1_scales[0])
+        dep_t = sb.tile([P, V], F32, name="dep_t")
+        gn_t = sb.tile([P, PACK], F32, name="gn_t")
+        nc.gpsimd.dma_start(out=gn_t[:], in_=gn.rearrange("(p t) o -> p (t o)", t=PACK))
+        nc.gpsimd.dma_start(out=dep_t[:], in_=dep.rearrange("(p t) v -> p t v", t=PACK)[:, 0, :])
+        w2_raw = sb.tile([P, 2 * N], U8, name="w2_raw")
+        nc.gpsimd.dma_start(out=w2_raw[:].bitcast(I32), in_=w2_words[0].bitcast(I32))
+        nc.sync.dma_start(i_t[:], i_l)
+        nc.sync.dma_start(j_t[:], j_l)
+        load_scale_rows([nc.sync] * 4, w2s_raw, w2_scales[0])
+        res_t = sb.tile([P, PACK, V], F32, name="res_t")
+        nc.sync.dma_start(out=res_t[:], in_=res.rearrange("(p t) v -> p t v", t=PACK))
+
+        one = sb.tile([P, 1], F32, name="one")
+        nc.scalar.activation(out=one[:], in_=zero[:], func=ACT.Exp)
+        gd = sb.tile([P, PACK, V], F32, name="gd")
+        for t in range(PACK):
+            nc.scalar.activation(out=gd[:, t, :], in_=dep_t[:], func=ACT.Copy, scale=gn_t[:, t : t + 1])
+
+        w1d = sb.tile([P, PACK, 2 * P], U8, name="w1d", align_bytes=64)
+        w1sd = sb.tile([P, PACK, P], U8, name="w1sd", align_bytes=64)
+        w2sd = sb.tile([P, PACK, P], U8, name="w2sd", align_bytes=64)
+        xsq = sb.tile([P, S], U8, name="xsq", align_bytes=64)
+
+        deal_words(nc, w1d, w_raw)
+        nc.vector.tensor_copy(out=xsq[:], in_=xs_raw[:].indirect(offs_t[:]))
+        deal_scales(nc, w1sd, w1s_raw)
+        xq = sb.tile([P, S], U32, name="xq", tag="w1s_xq", align_bytes=64)
+
+        y = [sb.tile([P, S], F32, name="y%d" % t) for t in range(PACK)]
+
+        def product1(t, cols, name):
+            acc = ps.tile([P, cols.stop - cols.start], F32, name=name)
+            nc.tensor.matmul_mx(
+                out=acc[:],
+                lhsT=w1d[:, t, :].bitcast(FP4X4),
+                lhsT_scale=w1sd[:, t, :],
+                rhs=xq[:, cols].bitcast(FP8X4),
+                rhs_scale=xsq[:, cols],
+                start=True,
+                stop=True,
+            )
+            nc.scalar.copy(out=y[t][:, cols], in_=acc[:])
+
+        for h in range(2):
+            cols = slice(h * SH, (h + 1) * SH)
+            nc.vector.tensor_copy(out=xq[:, cols], in_=xw[:].indirect(offs_t[:, h * SH // 16 : (h + 1) * SH // 16]))
+            for t in range(2):
+                product1(t, cols, "acc%d%d" % (t, h))
+        for t in range(2, PACK):
+            product1(t, slice(0, S), "acc%d" % t)
+
+        w2d = sb.tile([P, PACK, 2 * P], U8, name="w2d", tag="xw_w2d", align_bytes=64)
+        deal_words(nc, w2d, w2_raw)
+        deal_scales(nc, w2sd, w2s_raw)
+
+        sq = []
+        for h in range(2):
+            lc = slice(h * VH // 16, (h + 1) * VH // 16)
+            yi = sb.tile([P, PACK, VH], F32, name="yi%d" % h)
+            d = sb.tile([P, PACK, VH], F32, name="d%d" % h)
+            a = sb.tile([P, PACK, VH], F32, name="a%d" % h)
+            e = sb.tile([P, PACK, VH], F32, name="e%d" % h)
+            m2 = sb.tile([P, PACK, VH], F32, name="m2%d" % h)
+            groups = [(0, 2), (2, 4)] if h == 0 else [(0, 1), (1, 2), (2, 3), (3, 4)]
+            for lo, hi in groups:
+                for t in range(lo, hi):
+                    nc.vector.tensor_copy(out=yi[:, t, :], in_=y[t][:].indirect(i_t[:, lc]))
+                    nc.vector.tensor_tensor(out=d[:, t, :], in0=y[t][:].indirect(j_t[:, lc]), in1=yi[:, t, :], op=ALU.subtract)
+                nc.scalar.activation(out=a[:, lo:hi, :], in_=d[:, lo:hi, :], func=ACT.Abs)
+                nc.scalar.activation(out=e[:, lo:hi, :], in_=a[:, lo:hi, :], func=ACT.Exp, scale=-1.0)
+                nc.scalar.activation(out=m2[:, lo:hi, :], in_=e[:, lo:hi, :], func=ACT.Square, scale=-1.0, bias=one[:])
+            sq.append(m2)
+
+        acc2 = []
+        for h in range(2):
+            vc = slice(h * VH, (h + 1) * VH)
+            zb = sb.tile([P, VH, PACK], BF16, name="zb%d" % h, tag="slot%d" % h, align_bytes=64)
+            nc.vector.tensor_tensor(
+                out=zb[:].rearrange("p (c i) t -> p c t i", i=4),
+                in0=sq[h][:].rearrange("p t (c i) -> p c t i", i=4),
+                in1=gd[:, :, vc].rearrange("p t (c i) -> p c t i", i=4),
+                op=ALU.mult,
+            )
+            zq = sb.tile([P, VH], U32, name="zq%d" % h, align_bytes=64)
+            zs = sb.tile([P, VH], U8, name="zs%d" % h, align_bytes=64)
+            nc.vector.quantize_mx(out=zq[:].bitcast(FP8X4), scales=zs[:], in_=zb[:].rearrange("p v t -> p (v t)"))
+            acc = ps.tile([P, PACK, VH], F32, name="out%d" % h)
+            for t in range(PACK):
+                nc.tensor.matmul_mx(
+                    out=acc[:, t, :],
+                    lhsT=w2d[:, t, :].bitcast(FP4X4),
+                    lhsT_scale=w2sd[:, t, :],
+                    rhs=zq[:].bitcast(FP8X4),
+                    rhs_scale=zs[:],
+                    start=True,
+                    stop=True,
+                )
+            acc2.append(acc)
+
+        ow = sb.tile([P, V], U32, name="ow", align_bytes=64)
+        osc = sb.tile([P, V], U8, name="osc", align_bytes=64)
+        out_rows = out_0.rearrange("(p t) v -> p t v", t=PACK)
+        out_words = out_1[0].rearrange("p n t -> p (n t)").bitcast(I32)
+        for h in range(2):
+            vc = slice(h * VH, (h + 1) * VH)
+            o = sb.tile([P, PACK, VH], F32, name="o%d" % h, tag="slot%d" % (h + 1), align_bytes=64)
+            nc.vector.tensor_tensor(out=o[:], in0=acc2[h][:], in1=res_t[:, :, vc], op=ALU.add)
+            nc.sync.dma_start(out=out_rows[:, :, vc], in_=o[:])
+            ob = sb.tile([P, VH, PACK], BF16, name="ob%d" % h, align_bytes=64)
+            nc.scalar.copy(
+                out=ob[:].rearrange("p (c i) t -> p c t i", i=4),
+                in_=o[:].rearrange("p t (c i) -> p c t i", i=4),
+            )
+            nc.vector.quantize_mx(out=ow[:, vc].bitcast(FP8X4), scales=osc[:, vc], in_=ob[:].rearrange("p v t -> p (v t)"))
+            nc.sync.dma_start(out=out_words[:, vc], in_=ow[:, vc].bitcast(I32))
+        for q in range(4):
+            queue = nc.scalar if q % 2 == 0 else nc.sync
+            queue.dma_start(out=out_2[0, 4 * q : 4 * q + 4, :].bitcast(I32), in_=osc[32 * q : 32 * q + 4, :].bitcast(I32))

@@ -18,6 +18,7 @@ PACK = 4
 K, T, S, V, H, N = 512, 2048, 512, 256, 512, 512
 SH = S // 2
 VH = V // 2
+X_FIRST = 768
 FLOPS = 2 * K * H * S + 2 * H * N * V
 
 
@@ -53,105 +54,154 @@ def tile_picked_morse8_none_po_kernel(
         xs_raw = sb.tile([P, T], U8, name="xs_raw")
         w1s_raw = sb.tile([P, H], U8, name="w1s_raw", tag="w1s_xq", align_bytes=64)
         w2s_raw = sb.tile([P, N], U8, name="w2s_raw")
-        zero = sb.tile([P, 1], F32, name="zero")
+        zero = sb.tile([P, 1], F32, name="zero", tag="zero_d")
         nc.vector.memset(xs_raw[:].bitcast(I32), 0)
-        nc.gpsimd.memset(w1s_raw[:].bitcast(I32), 0)
-        nc.vector.memset(w2s_raw[:].bitcast(I32), 0)
+        nc.vector.memset(w1s_raw[:].bitcast(I32), 0)
+        nc.gpsimd.memset(w2s_raw[:].bitcast(I32), 0)
         nc.vector.memset(zero[:], 0.0)
 
         xw = sb.tile([P, T], U32, name="xw", tag="xw_w2d", align_bytes=64)
-        w_raw = sb.tile([P, 2 * H], U8, name="w_raw")
-        nc.sync.dma_start(offs_t[:], offs)
-        nc.sync.dma_start(out=w_raw[:].bitcast(I32), in_=w1_words[0].bitcast(I32))
-        nc.sync.dma_start(out=xw[:].bitcast(I32), in_=x_words[0].rearrange("p n t -> p (n t)").bitcast(I32))
-        load_scale_rows([nc.scalar] * 4, xs_raw, x_scales[0])
-        load_scale_rows([nc.scalar] * 3 + [nc.gpsimd], w1s_raw, w1_scales[0])
-        dep_t = sb.tile([P, V], F32, name="dep_t")
-        gn_t = sb.tile([P, PACK], F32, name="gn_t")
-        nc.gpsimd.dma_start(out=gn_t[:], in_=gn.rearrange("(p t) o -> p (t o)", t=PACK))
-        nc.gpsimd.dma_start(out=dep_t[:], in_=dep.rearrange("(p t) v -> p t v", t=PACK)[:, 0, :])
+        w_raw = sb.tile([P, 2 * H], U8, name="w_raw", tag="w1_dep")
         w2_raw = sb.tile([P, 2 * N], U8, name="w2_raw")
-        nc.gpsimd.dma_start(out=w2_raw[:].bitcast(I32), in_=w2_words[0].bitcast(I32))
+        res_t = sb.tile([P, PACK, V], F32, name="res_t")
+        x_rows = x_words[0].rearrange("p n t -> p (n t)").bitcast(I32)
+        nc.sync.dma_start(offs_t[:], offs)
+        nc.scalar.dma_start(out=w_raw[:].bitcast(I32), in_=w1_words[0].bitcast(I32))
+        nc.sync.dma_start(out=xw[:, :X_FIRST].bitcast(I32), in_=x_rows[:, :X_FIRST])
+        load_scale_rows([nc.sync] * 2 + [nc.scalar] * 2, xs_raw, x_scales[0])
+        nc.sync.dma_start(out=xw[:, X_FIRST:].bitcast(I32), in_=x_rows[:, X_FIRST:])
+        load_scale_rows([nc.sync] * 4, w1s_raw, w1_scales[0])
+        nc.sync.dma_start(out=w2_raw[:].bitcast(I32), in_=w2_words[0].bitcast(I32))
         nc.sync.dma_start(i_t[:], i_l)
         nc.sync.dma_start(j_t[:], j_l)
-        load_scale_rows([nc.sync] * 4, w2s_raw, w2_scales[0])
-        res_t = sb.tile([P, PACK, V], F32, name="res_t")
+        load_scale_rows([nc.gpsimd] * 4, w2s_raw, w2_scales[0])
         nc.sync.dma_start(out=res_t[:], in_=res.rearrange("(p t) v -> p t v", t=PACK))
 
         one = sb.tile([P, 1], F32, name="one")
         nc.scalar.activation(out=one[:], in_=zero[:], func=ACT.Exp)
+        gn_t = sb.tile([P, PACK], F32, name="gn_t")
+        nc.gpsimd.dma_start(out=gn_t[:], in_=gn.rearrange("(p t) o -> p (t o)", t=PACK))
+
+        w1d = sb.tile([P, PACK, 2 * P], U8, name="w1d", align_bytes=64)
+        w1sd = sb.tile([P, PACK, P], U8, name="w1sd", align_bytes=64)
+        xsq = sb.tile([P, S], U8, name="xsq", align_bytes=64)
+
+        deal_words(nc, w1d, w_raw)
+        dep_t = sb.tile([P, V], F32, name="dep_t", tag="w1_dep")
+        nc.scalar.dma_start(out=dep_t[:], in_=dep.rearrange("(p t) v -> p t v", t=PACK)[:, 0, :])
+        nc.vector.tensor_copy(out=xsq[:], in_=xs_raw[:].indirect(offs_t[:]))
+
+        y = [sb.tile([P, S], F32, name="y%d" % t) for t in range(PACK)]
+        xq = []
+
+        def gather_words(h, tag):
+            words = sb.tile([P, SH], U32, name="xq%d" % h, tag=tag, align_bytes=64)
+            nc.vector.tensor_copy(out=words[:], in_=xw[:].indirect(offs_t[:, h * SH // 16 : (h + 1) * SH // 16]))
+            xq.append(words)
+
+        def product1(acc, t, h):
+            nc.tensor.matmul_mx(
+                out=acc,
+                lhsT=w1d[:, t, :].bitcast(FP4X4),
+                lhsT_scale=w1sd[:, t, :],
+                rhs=xq[h][:].bitcast(FP8X4),
+                rhs_scale=xsq[:, h * SH : (h + 1) * SH],
+                start=True,
+                stop=True,
+            )
+
+        gather_words(0, "xq0")
+        deal_scales(nc, w1sd, w1s_raw)
+        gather_words(1, "w1s_xq")
+        for h in range(2):
+            for t in range(2):
+                acc = ps.tile([P, SH], F32, name="acc%d%d" % (t, h))
+                product1(acc[:], t, h)
+                if h == 1 and t == 1:
+                    nc.vector.tensor_copy(out=y[t][:, h * SH : (h + 1) * SH], in_=acc[:])
+                else:
+                    nc.scalar.copy(out=y[t][:, h * SH : (h + 1) * SH], in_=acc[:])
+        for t in range(2, PACK):
+            acc = ps.tile([P, S], F32, name="acc%d" % t)
+            for h in range(2):
+                product1(acc[:, h * SH : (h + 1) * SH], t, h)
+            if t == 2:
+                nc.scalar.copy(out=y[t][:], in_=acc[:])
+            else:
+                nc.scalar.activation(out=y[t][:], in_=acc[:], func=ACT.Identity, bias=zero[:])
+
+        w2d = sb.tile([P, PACK, 2 * P], U8, name="w2d", tag="xw_w2d", align_bytes=64)
+        deal_words(nc, w2d, w2_raw)
+
         gd = sb.tile([P, PACK, V], F32, name="gd")
         for t in range(PACK):
             nc.scalar.activation(out=gd[:, t, :], in_=dep_t[:], func=ACT.Copy, scale=gn_t[:, t : t + 1])
 
-        w1d = sb.tile([P, PACK, 2 * P], U8, name="w1d", align_bytes=64)
-        w1sd = sb.tile([P, PACK, P], U8, name="w1sd", align_bytes=64)
-        w2sd = sb.tile([P, PACK, P], U8, name="w2sd", align_bytes=64)
-        xsq = sb.tile([P, S], U8, name="xsq", align_bytes=64)
+        def offsets(lst, h):
+            return lst[:, h * VH // 16 : (h + 1) * VH // 16]
 
-        deal_words(nc, w1d, w_raw)
-        nc.vector.tensor_copy(out=xsq[:], in_=xs_raw[:].indirect(offs_t[:]))
-        deal_scales(nc, w1sd, w1s_raw)
-        xq = sb.tile([P, S], U32, name="xq", tag="w1s_xq", align_bytes=64)
+        sq = [sb.tile([P, PACK, VH], F32, name="m2%d" % h) for h in range(2)]
+        items = [(h, t) for h in range(2) for t in range(PACK)]
+        yi, d, a, e = {}, {}, {}, {}
 
-        y = [sb.tile([P, S], F32, name="y%d" % t) for t in range(PACK)]
+        def fetch_i(k):
+            h, t = items[k]
+            yi[k] = sb.tile([P, VH], F32, name="yi%d" % k, tag="yi%d" % (k % 2), align_bytes=64)
+            nc.vector.tensor_copy(out=yi[k][:], in_=y[t][:].indirect(offsets(i_t, h)))
 
-        def product1(t, cols, name):
-            acc = ps.tile([P, cols.stop - cols.start], F32, name=name)
-            nc.tensor.matmul_mx(
-                out=acc[:],
-                lhsT=w1d[:, t, :].bitcast(FP4X4),
-                lhsT_scale=w1sd[:, t, :],
-                rhs=xq[:, cols].bitcast(FP8X4),
-                rhs_scale=xsq[:, cols],
-                start=True,
-                stop=True,
-            )
-            nc.scalar.copy(out=y[t][:, cols], in_=acc[:])
+        def minus_j(k):
+            h, t = items[k]
+            d[k] = sb.tile([P, VH], F32, name="d%d" % k, tag="zero_d" if k == 2 else "d%d" % k)
+            nc.vector.tensor_tensor(out=d[k][:], in0=y[t][:].indirect(offsets(j_t, h)), in1=yi[k][:], op=ALU.subtract)
 
-        for h in range(2):
-            cols = slice(h * SH, (h + 1) * SH)
-            nc.vector.tensor_copy(out=xq[:, cols], in_=xw[:].indirect(offs_t[:, h * SH // 16 : (h + 1) * SH // 16]))
-            for t in range(2):
-                product1(t, cols, "acc%d%d" % (t, h))
-        for t in range(2, PACK):
-            product1(t, slice(0, S), "acc%d" % t)
+        def size(k):
+            a[k] = sb.tile([P, VH], F32, name="a%d" % k, tag="a", bufs=2)
+            nc.scalar.activation(out=a[k][:], in_=d[k][:], func=ACT.Abs)
 
-        w2d = sb.tile([P, PACK, 2 * P], U8, name="w2d", tag="xw_w2d", align_bytes=64)
-        deal_words(nc, w2d, w2_raw)
+        def decay(k):
+            e[k] = sb.tile([P, VH], F32, name="e%d" % k, tag="e", bufs=2)
+            nc.scalar.activation(out=e[k][:], in_=a[k][:], func=ACT.Exp, scale=-1.0)
+
+        def square(k):
+            h, t = items[k]
+            nc.scalar.activation(out=sq[h][:, t, :], in_=e[k][:], func=ACT.Square, scale=-1.0, bias=one[:])
+
+        for k in range(0, len(items), 2):
+            fetch_i(k)
+            fetch_i(k + 1)
+            minus_j(k)
+            minus_j(k + 1)
+            for n in (k, k + 1):
+                size(n)
+                if n >= 2:
+                    square(n - 2)
+            decay(k)
+            decay(k + 1)
+        square(len(items) - 2)
+        square(len(items) - 1)
+
+        w2sd = sb.tile([P, PACK, P], U8, name="w2sd", tag="yi1", align_bytes=64)
         deal_scales(nc, w2sd, w2s_raw)
 
-        sq = []
-        for h in range(2):
-            lc = slice(h * VH // 16, (h + 1) * VH // 16)
-            yi = sb.tile([P, PACK, VH], F32, name="yi%d" % h)
-            d = sb.tile([P, PACK, VH], F32, name="d%d" % h)
-            a = sb.tile([P, PACK, VH], F32, name="a%d" % h)
-            e = sb.tile([P, PACK, VH], F32, name="e%d" % h)
-            m2 = sb.tile([P, PACK, VH], F32, name="m2%d" % h)
-            groups = [(0, 2), (2, 4)] if h == 0 else [(0, 1), (1, 2), (2, 3), (3, 4)]
-            for lo, hi in groups:
-                for t in range(lo, hi):
-                    nc.vector.tensor_copy(out=yi[:, t, :], in_=y[t][:].indirect(i_t[:, lc]))
-                    nc.vector.tensor_tensor(out=d[:, t, :], in0=y[t][:].indirect(j_t[:, lc]), in1=yi[:, t, :], op=ALU.subtract)
-                nc.scalar.activation(out=a[:, lo:hi, :], in_=d[:, lo:hi, :], func=ACT.Abs)
-                nc.scalar.activation(out=e[:, lo:hi, :], in_=a[:, lo:hi, :], func=ACT.Exp, scale=-1.0)
-                nc.scalar.activation(out=m2[:, lo:hi, :], in_=e[:, lo:hi, :], func=ACT.Square, scale=-1.0, bias=one[:])
-            sq.append(m2)
+        def pieces(h):
+            return [slice(0, VH)] if h == 0 else [slice(0, VH // 2), slice(VH // 2, VH)]
+
+        def by_word(ap):
+            return ap.rearrange("p (c i) t -> p c t i", i=4)
+
+        def by_row(ap):
+            return ap.rearrange("p t (c i) -> p c t i", i=4)
 
         acc2 = []
         for h in range(2):
-            vc = slice(h * VH, (h + 1) * VH)
             zb = sb.tile([P, VH, PACK], BF16, name="zb%d" % h, tag="slot%d" % h, align_bytes=64)
-            nc.vector.tensor_tensor(
-                out=zb[:].rearrange("p (c i) t -> p c t i", i=4),
-                in0=sq[h][:].rearrange("p t (c i) -> p c t i", i=4),
-                in1=gd[:, :, vc].rearrange("p t (c i) -> p c t i", i=4),
-                op=ALU.mult,
-            )
             zq = sb.tile([P, VH], U32, name="zq%d" % h, align_bytes=64)
             zs = sb.tile([P, VH], U8, name="zs%d" % h, align_bytes=64)
-            nc.vector.quantize_mx(out=zq[:].bitcast(FP8X4), scales=zs[:], in_=zb[:].rearrange("p v t -> p (v t)"))
+            for c in pieces(h):
+                vc = slice(h * VH + c.start, h * VH + c.stop)
+                nc.vector.tensor_tensor(out=by_word(zb[:, c, :]), in0=by_row(sq[h][:, :, c]), in1=by_row(gd[:, :, vc]), op=ALU.mult)
+            for c in pieces(h):
+                nc.vector.quantize_mx(out=zq[:, c].bitcast(FP8X4), scales=zs[:, c], in_=zb[:, c, :].rearrange("p v t -> p (v t)"))
             acc = ps.tile([P, PACK, VH], F32, name="out%d" % h)
             for t in range(PACK):
                 nc.tensor.matmul_mx(
@@ -172,14 +222,15 @@ def tile_picked_morse8_none_po_kernel(
         for h in range(2):
             vc = slice(h * VH, (h + 1) * VH)
             o = sb.tile([P, PACK, VH], F32, name="o%d" % h, tag="slot%d" % (h + 1), align_bytes=64)
-            nc.vector.tensor_tensor(out=o[:], in0=acc2[h][:], in1=res_t[:, :, vc], op=ALU.add)
-            nc.sync.dma_start(out=out_rows[:, :, vc], in_=o[:])
             ob = sb.tile([P, VH, PACK], BF16, name="ob%d" % h, align_bytes=64)
-            nc.scalar.copy(
-                out=ob[:].rearrange("p (c i) t -> p c t i", i=4),
-                in_=o[:].rearrange("p t (c i) -> p c t i", i=4),
-            )
-            nc.vector.quantize_mx(out=ow[:, vc].bitcast(FP8X4), scales=osc[:, vc], in_=ob[:].rearrange("p v t -> p (v t)"))
+            for c in pieces(h):
+                pc = slice(h * VH + c.start, h * VH + c.stop)
+                nc.vector.tensor_tensor(out=o[:, :, c], in0=acc2[h][:, :, c], in1=res_t[:, :, pc], op=ALU.add)
+                nc.scalar.copy(out=by_word(ob[:, c, :]), in_=by_row(o[:, :, c]))
+            nc.sync.dma_start(out=out_rows[:, :, vc], in_=o[:])
+            for c in pieces(h):
+                pc = slice(h * VH + c.start, h * VH + c.stop)
+                nc.vector.quantize_mx(out=ow[:, pc].bitcast(FP8X4), scales=osc[:, pc], in_=ob[:, c, :].rearrange("p v t -> p (v t)"))
             nc.sync.dma_start(out=out_words[:, vc], in_=ow[:, vc].bitcast(I32))
         for q in range(4):
             queue = nc.scalar if q % 2 == 0 else nc.sync

@@ -18,7 +18,7 @@ PACK = 4
 K, T, S, V, H, N = 512, 2048, 512, 256, 512, 512
 SH = S // 2
 VH = V // 2
-X_FIRST = 768
+X_FIRST = 512
 FLOPS = 2 * K * H * S + 2 * H * N * V
 
 
@@ -29,8 +29,8 @@ def load_scale_rows(queues, plane, rows):
 
 def deal_words(nc, dealt, raw):
     nc.vector.tensor_copy(
-        out=dealt[:].rearrange("p t (m b) -> p t m b", b=2),
-        in_=raw[:].rearrange("p (m t b) -> p t m b", t=PACK, b=2),
+        out=dealt[:].bitcast(U16),
+        in_=raw[:].bitcast(U16).rearrange("p (m t) -> p t m", t=PACK),
     )
 
 
@@ -57,7 +57,7 @@ def tile_picked_morse8_none_po_kernel(
         zero = sb.tile([P, 1], F32, name="zero", tag="zero_d")
         nc.vector.memset(xs_raw[:].bitcast(I32), 0)
         nc.vector.memset(w1s_raw[:].bitcast(I32), 0)
-        nc.gpsimd.memset(w2s_raw[:].bitcast(I32), 0)
+        nc.vector.memset(w2s_raw[:].bitcast(I32), 0)
         nc.vector.memset(zero[:], 0.0)
 
         xw = sb.tile([P, T], U32, name="xw", tag="xw_w2d", align_bytes=64)
@@ -74,7 +74,7 @@ def tile_picked_morse8_none_po_kernel(
         nc.sync.dma_start(out=w2_raw[:].bitcast(I32), in_=w2_words[0].bitcast(I32))
         nc.sync.dma_start(i_t[:], i_l)
         nc.sync.dma_start(j_t[:], j_l)
-        load_scale_rows([nc.gpsimd] * 4, w2s_raw, w2_scales[0])
+        load_scale_rows([nc.sync] * 4, w2s_raw, w2_scales[0])
         nc.sync.dma_start(out=res_t[:], in_=res.rearrange("(p t) v -> p t v", t=PACK))
 
         one = sb.tile([P, 1], F32, name="one")
@@ -115,7 +115,7 @@ def tile_picked_morse8_none_po_kernel(
         gather_words(1, "w1s_xq")
         for h in range(2):
             for t in range(2):
-                acc = ps.tile([P, SH], F32, name="acc%d%d" % (t, h))
+                acc = ps.tile([P, SH], F32, name="acc%d%d" % (t, h), tag="acc%d%d" % (t, h))
                 product1(acc[:], t, h)
                 if h == 1 and t == 1:
                     nc.vector.tensor_copy(out=y[t][:, h * SH : (h + 1) * SH], in_=acc[:])
@@ -202,18 +202,21 @@ def tile_picked_morse8_none_po_kernel(
                 nc.vector.tensor_tensor(out=by_word(zb[:, c, :]), in0=by_row(sq[h][:, :, c]), in1=by_row(gd[:, :, vc]), op=ALU.mult)
             for c in pieces(h):
                 nc.vector.quantize_mx(out=zq[:, c].bitcast(FP8X4), scales=zs[:, c], in_=zb[:, c, :].rearrange("p v t -> p (v t)"))
-            acc = ps.tile([P, PACK, VH], F32, name="out%d" % h)
-            for t in range(PACK):
-                nc.tensor.matmul_mx(
-                    out=acc[:, t, :],
-                    lhsT=w2d[:, t, :].bitcast(FP4X4),
-                    lhsT_scale=w2sd[:, t, :],
-                    rhs=zq[:].bitcast(FP8X4),
-                    rhs_scale=zs[:],
-                    start=True,
-                    stop=True,
-                )
-            acc2.append(acc)
+            banks = []
+            for u in range(2):
+                acc = ps.tile([P, 2, VH], F32, name="out%d%d" % (h, u), tag="acc%d%d" % (u, h))
+                for t in range(2 * u, 2 * u + 2):
+                    nc.tensor.matmul_mx(
+                        out=acc[:, t - 2 * u, :],
+                        lhsT=w2d[:, t, :].bitcast(FP4X4),
+                        lhsT_scale=w2sd[:, t, :],
+                        rhs=zq[:].bitcast(FP8X4),
+                        rhs_scale=zs[:],
+                        start=True,
+                        stop=True,
+                    )
+                banks.append(acc)
+            acc2.append(banks)
 
         ow = sb.tile([P, V], U32, name="ow", align_bytes=64)
         osc = sb.tile([P, V], U8, name="osc", align_bytes=64)
@@ -223,10 +226,14 @@ def tile_picked_morse8_none_po_kernel(
             vc = slice(h * VH, (h + 1) * VH)
             o = sb.tile([P, PACK, VH], F32, name="o%d" % h, tag="slot%d" % (h + 1), align_bytes=64)
             ob = sb.tile([P, VH, PACK], BF16, name="ob%d" % h, align_bytes=64)
+            for u in range(2):
+                ts = slice(2 * u, 2 * u + 2)
+                nc.vector.tensor_tensor(out=o[:, ts, :], in0=acc2[h][u][:], in1=res_t[:, ts, vc], op=ALU.add)
             for c in pieces(h):
-                pc = slice(h * VH + c.start, h * VH + c.stop)
-                nc.vector.tensor_tensor(out=o[:, :, c], in0=acc2[h][:, :, c], in1=res_t[:, :, pc], op=ALU.add)
-                nc.scalar.copy(out=by_word(ob[:, c, :]), in_=by_row(o[:, :, c]))
+                if c.start == 0:
+                    nc.scalar.copy(out=by_word(ob[:, c, :]), in_=by_row(o[:, :, c]))
+                else:
+                    nc.vector.tensor_copy(out=by_word(ob[:, c, :]), in_=by_row(o[:, :, c]))
             nc.sync.dma_start(out=out_rows[:, :, vc], in_=o[:])
             for c in pieces(h):
                 pc = slice(h * VH + c.start, h * VH + c.stop)

@@ -51,26 +51,35 @@ def tile_picked_morse8_none_po_kernel(
         i_t = lists.tile([P, V // 16], U16, name="i_t")
         j_t = lists.tile([P, V // 16], U16, name="j_t")
 
-        xs_raw = sb.tile([P, T], U8, name="xs_raw")
-        w1s_raw = sb.tile([P, H], U8, name="w1s_raw", tag="w1s_xq", align_bytes=64)
+        xs_raw = sb.tile([P, T], U8, name="xs_raw", tag="xs_w1d", align_bytes=64)
+        w1s_raw = sb.tile([P, H], U8, name="w1s_raw")
         w2s_raw = sb.tile([P, N], U8, name="w2s_raw")
         zero = sb.tile([P, 1], F32, name="zero", tag="zero_d")
         nc.vector.memset(xs_raw[:].bitcast(I32), 0)
         nc.vector.memset(w1s_raw[:].bitcast(I32), 0)
         nc.vector.memset(w2s_raw[:].bitcast(I32), 0)
+        xsd = sb.tile([P, S], U8, name="xsd", align_bytes=64)
+        nc.vector.memset(xsd[:].bitcast(I32), 0)
         nc.vector.memset(zero[:], 0.0)
 
         xw = sb.tile([P, T], U32, name="xw", tag="xw_w2d", align_bytes=64)
-        w_raw = sb.tile([P, 2 * H], U8, name="w_raw", tag="w1_dep")
+        w_raw = sb.tile([P, 2 * H], U8, name="w_raw")
         w2_raw = sb.tile([P, 2 * N], U8, name="w2_raw")
         res_t = sb.tile([P, PACK, V], F32, name="res_t")
         x_rows = x_words[0].rearrange("p n t -> p (n t)").bitcast(I32)
+        dep_t = sb.tile([P, V], F32, name="dep_t")
+        xsq = sb.tile([P, S], U8, name="xsq")
         nc.sync.dma_start(offs_t[:], offs)
-        nc.scalar.dma_start(out=w_raw[:].bitcast(I32), in_=w1_words[0].bitcast(I32))
+        nc.gpsimd.dma_start(out=w_raw[:].bitcast(I32), in_=w1_words[0].bitcast(I32))
         nc.sync.dma_start(out=xw[:, :X_FIRST].bitcast(I32), in_=x_rows[:, :X_FIRST])
-        load_scale_rows([nc.sync] * 2 + [nc.scalar] * 2, xs_raw, x_scales[0])
+        nc.sync.dma_start(out=xs_raw[0:P:8, :].bitcast(I32), in_=x_scales[0].bitcast(I32))
+        load_scale_rows([nc.scalar] * 2 + [nc.sync] * 2, w1s_raw, w1_scales[0])
         nc.sync.dma_start(out=xw[:, X_FIRST:].bitcast(I32), in_=x_rows[:, X_FIRST:])
-        load_scale_rows([nc.sync] * 4, w1s_raw, w1_scales[0])
+        nc.sync.dma_start(out=dep_t[:], in_=dep.rearrange("(p t) v -> p t v", t=PACK)[:, 0, :])
+        nc.vector.tensor_copy(out=xsq[:], in_=xs_raw[:].indirect(offs_t[:]))
+        for q in range(4):
+            queue = nc.sync if q < 2 else nc.scalar
+            queue.dma_start(out=xsd[32 * q : 32 * q + 4, :].bitcast(I32), in_=xsq[32 * q : 32 * q + 32 : 8, :].bitcast(I32))
         nc.sync.dma_start(out=w2_raw[:].bitcast(I32), in_=w2_words[0].bitcast(I32))
         nc.sync.dma_start(i_t[:], i_l)
         nc.sync.dma_start(j_t[:], j_l)
@@ -82,14 +91,11 @@ def tile_picked_morse8_none_po_kernel(
         gn_t = sb.tile([P, PACK], F32, name="gn_t")
         nc.gpsimd.dma_start(out=gn_t[:], in_=gn.rearrange("(p t) o -> p (t o)", t=PACK))
 
-        w1d = sb.tile([P, PACK, 2 * P], U8, name="w1d", align_bytes=64)
+        w1d = sb.tile([P, PACK, 2 * P], U8, name="w1d", tag="xs_w1d", align_bytes=64)
         w1sd = sb.tile([P, PACK, P], U8, name="w1sd", align_bytes=64)
-        xsq = sb.tile([P, S], U8, name="xsq", align_bytes=64)
 
         deal_words(nc, w1d, w_raw)
-        dep_t = sb.tile([P, V], F32, name="dep_t", tag="w1_dep")
-        nc.scalar.dma_start(out=dep_t[:], in_=dep.rearrange("(p t) v -> p t v", t=PACK)[:, 0, :])
-        nc.vector.tensor_copy(out=xsq[:], in_=xs_raw[:].indirect(offs_t[:]))
+        deal_scales(nc, w1sd, w1s_raw)
 
         y = [sb.tile([P, S], F32, name="y%d" % t) for t in range(PACK)]
         xq = []
@@ -105,14 +111,13 @@ def tile_picked_morse8_none_po_kernel(
                 lhsT=w1d[:, t, :].bitcast(FP4X4),
                 lhsT_scale=w1sd[:, t, :],
                 rhs=xq[h][:].bitcast(FP8X4),
-                rhs_scale=xsq[:, h * SH : (h + 1) * SH],
+                rhs_scale=xsd[:, h * SH : (h + 1) * SH],
                 start=True,
                 stop=True,
             )
 
         gather_words(0, "xq0")
-        deal_scales(nc, w1sd, w1s_raw)
-        gather_words(1, "w1s_xq")
+        gather_words(1, "xq1")
         for h in range(2):
             for t in range(2):
                 acc = ps.tile([P, SH], F32, name="acc%d%d" % (t, h), tag="acc%d%d" % (t, h))

from contextlib import ExitStack

import concourse.mybir as mybir

F32 = mybir.dt.float32
BF16 = mybir.dt.bfloat16
I32 = mybir.dt.int32
U32 = mybir.dt.uint32
U16 = mybir.dt.uint16
U8 = mybir.dt.uint8
FP8X4 = mybir.dt.float8_e4m3fn_x4
FP4X4 = mybir.dt.float4_e2m1fn_x4
ACT = mybir.ActivationFunctionType
ALU = mybir.AluOpType

P = 128
PACK = 4
K, T, S, V, H, N = 512, 2048, 512, 256, 512, 512
SH = S // 2
VH = V // 2
X_FIRST = 512
FLOPS = 2 * K * H * S + 2 * H * N * V


def load_scale_rows(queues, plane, rows):
    for q in range(4):
        queues[q].dma_start(out=plane[32 * q : 32 * q + 4, :].bitcast(I32), in_=rows[4 * q : 4 * q + 4, :].bitcast(I32))


def deal_words(nc, dealt, raw):
    nc.vector.tensor_copy(
        out=dealt[:].bitcast(U16),
        in_=raw[:].bitcast(U16).rearrange("p (m t) -> p t m", t=PACK),
    )


def deal_scales(nc, dealt, raw):
    nc.vector.tensor_copy(out=dealt[:], in_=raw[:].rearrange("p (m t) -> p t m", t=PACK))


def tile_picked_morse8_none_po_kernel(
    tc, x_words, x_scales, w1_words, w1_scales, dep, gn, w2_words, w2_scales, res, offs, i_l, j_l, out_0, out_1, out_2
):
    nc = tc.nc
    with ExitStack() as ctx:
        lists = ctx.enter_context(tc.tile_pool(name="lists", bufs=1))
        sb = ctx.enter_context(tc.tile_pool(name="sb", bufs=1))
        ps = ctx.enter_context(tc.psum_pool(name="ps", bufs=1))

        offs_t = lists.tile([P, S // 16], U16, name="offs_t")
        i_t = lists.tile([P, V // 16], U16, name="i_t")
        j_t = lists.tile([P, V // 16], U16, name="j_t")

        xs_raw = sb.tile([P, T], U8, name="xs_raw", tag="xs_w1d", align_bytes=64)
        w1s_raw = sb.tile([P, H], U8, name="w1s_raw")
        w2s_raw = sb.tile([P, N], U8, name="w2s_raw")
        zero = sb.tile([P, 1], F32, name="zero", tag="zero_d")
        nc.vector.memset(xs_raw[:].bitcast(I32), 0)
        nc.vector.memset(w1s_raw[:].bitcast(I32), 0)
        nc.vector.memset(w2s_raw[:].bitcast(I32), 0)
        xsd = sb.tile([P, S], U8, name="xsd", align_bytes=64)
        nc.vector.memset(xsd[:].bitcast(I32), 0)
        nc.vector.memset(zero[:], 0.0)

        xw = sb.tile([P, T], U32, name="xw", tag="xw_w2d", align_bytes=64)
        w_raw = sb.tile([P, 2 * H], U8, name="w_raw")
        w2_raw = sb.tile([P, 2 * N], U8, name="w2_raw")
        res_t = sb.tile([P, PACK, V], F32, name="res_t")
        x_rows = x_words[0].rearrange("p n t -> p (n t)").bitcast(I32)
        dep_t = sb.tile([P, V], F32, name="dep_t")
        xsq = sb.tile([P, S], U8, name="xsq")
        nc.sync.dma_start(offs_t[:], offs)
        nc.gpsimd.dma_start(out=w_raw[:].bitcast(I32), in_=w1_words[0].bitcast(I32))
        nc.sync.dma_start(out=xw[:, :X_FIRST].bitcast(I32), in_=x_rows[:, :X_FIRST])
        nc.sync.dma_start(out=xs_raw[0:P:8, :].bitcast(I32), in_=x_scales[0].bitcast(I32))
        load_scale_rows([nc.scalar] * 2 + [nc.sync] * 2, w1s_raw, w1_scales[0])
        nc.sync.dma_start(out=xw[:, X_FIRST:].bitcast(I32), in_=x_rows[:, X_FIRST:])
        nc.sync.dma_start(out=dep_t[:], in_=dep.rearrange("(p t) v -> p t v", t=PACK)[:, 0, :])
        nc.vector.tensor_copy(out=xsq[:], in_=xs_raw[:].indirect(offs_t[:]))
        for q in range(4):
            queue = nc.sync if q < 2 else nc.scalar
            queue.dma_start(out=xsd[32 * q : 32 * q + 4, :].bitcast(I32), in_=xsq[32 * q : 32 * q + 32 : 8, :].bitcast(I32))
        nc.sync.dma_start(out=w2_raw[:].bitcast(I32), in_=w2_words[0].bitcast(I32))
        nc.sync.dma_start(i_t[:], i_l)
        nc.sync.dma_start(j_t[:], j_l)
        load_scale_rows([nc.sync] * 4, w2s_raw, w2_scales[0])
        nc.sync.dma_start(out=res_t[:], in_=res.rearrange("(p t) v -> p t v", t=PACK))

        one = sb.tile([P, 1], F32, name="one")
        nc.scalar.activation(out=one[:], in_=zero[:], func=ACT.Exp)
        gn_t = sb.tile([P, PACK], F32, name="gn_t")
        nc.gpsimd.dma_start(out=gn_t[:], in_=gn.rearrange("(p t) o -> p (t o)", t=PACK))

        w1d = sb.tile([P, PACK, 2 * P], U8, name="w1d", tag="xs_w1d", align_bytes=64)
        w1sd = sb.tile([P, PACK, P], U8, name="w1sd", align_bytes=64)

        deal_words(nc, w1d, w_raw)
        deal_scales(nc, w1sd, w1s_raw)

        y = [sb.tile([P, S], F32, name="y%d" % t) for t in range(PACK)]
        xq = []

        def gather_words(h, tag):
            words = sb.tile([P, SH], U32, name="xq%d" % h, tag=tag, align_bytes=64)
            nc.vector.tensor_copy(out=words[:], in_=xw[:].indirect(offs_t[:, h * SH // 16 : (h + 1) * SH // 16]))
            xq.append(words)

        def product1(acc, t, h):
            nc.tensor.matmul_mx(
                out=acc,
                lhsT=w1d[:, t, :].bitcast(FP4X4),
                lhsT_scale=w1sd[:, t, :],
                rhs=xq[h][:].bitcast(FP8X4),
                rhs_scale=xsd[:, h * SH : (h + 1) * SH],
                start=True,
                stop=True,
            )

        gather_words(0, "xq0")
        gather_words(1, "xq1")
        for h in range(2):
            for t in range(2):
                acc = ps.tile([P, SH], F32, name="acc%d%d" % (t, h), tag="acc%d%d" % (t, h))
                product1(acc[:], t, h)
                if h == 1 and t == 1:
                    nc.vector.tensor_copy(out=y[t][:, h * SH : (h + 1) * SH], in_=acc[:])
                else:
                    nc.scalar.copy(out=y[t][:, h * SH : (h + 1) * SH], in_=acc[:])
        for t in range(2, PACK):
            acc = ps.tile([P, S], F32, name="acc%d" % t)
            for h in range(2):
                product1(acc[:, h * SH : (h + 1) * SH], t, h)
            if t == 2:
                nc.scalar.copy(out=y[t][:], in_=acc[:])
            else:
                nc.scalar.activation(out=y[t][:], in_=acc[:], func=ACT.Identity, bias=zero[:])

        w2d = sb.tile([P, PACK, 2 * P], U8, name="w2d", tag="xw_w2d", align_bytes=64)
        deal_words(nc, w2d, w2_raw)

        gd = sb.tile([P, PACK, V], F32, name="gd")
        for t in range(PACK):
            nc.scalar.activation(out=gd[:, t, :], in_=dep_t[:], func=ACT.Copy, scale=gn_t[:, t : t + 1])

        def offsets(lst, h):
            return lst[:, h * VH // 16 : (h + 1) * VH // 16]

        sq = [sb.tile([P, PACK, VH], F32, name="m2%d" % h) for h in range(2)]
        items = [(h, t) for h in range(2) for t in range(PACK)]
        yi, d, a, e = {}, {}, {}, {}

        def fetch_i(k):
            h, t = items[k]
            yi[k] = sb.tile([P, VH], F32, name="yi%d" % k, tag="yi%d" % (k % 2), align_bytes=64)
            nc.vector.tensor_copy(out=yi[k][:], in_=y[t][:].indirect(offsets(i_t, h)))

        def minus_j(k):
            h, t = items[k]
            d[k] = sb.tile([P, VH], F32, name="d%d" % k, tag="zero_d" if k == 2 else "d%d" % k)
            nc.vector.tensor_tensor(out=d[k][:], in0=y[t][:].indirect(offsets(j_t, h)), in1=yi[k][:], op=ALU.subtract)

        def size(k):
            a[k] = sb.tile([P, VH], F32, name="a%d" % k, tag="a", bufs=2)
            nc.scalar.activation(out=a[k][:], in_=d[k][:], func=ACT.Abs)

        def decay(k):
            e[k] = sb.tile([P, VH], F32, name="e%d" % k, tag="e", bufs=2)
            nc.scalar.activation(out=e[k][:], in_=a[k][:], func=ACT.Exp, scale=-1.0)

        def square(k):
            h, t = items[k]
            nc.scalar.activation(out=sq[h][:, t, :], in_=e[k][:], func=ACT.Square, scale=-1.0, bias=one[:])

        for k in range(0, len(items), 2):
            fetch_i(k)
            fetch_i(k + 1)
            minus_j(k)
            minus_j(k + 1)
            for n in (k, k + 1):
                size(n)
                if n >= 2:
                    square(n - 2)
            decay(k)
            decay(k + 1)
        square(len(items) - 2)
        square(len(items) - 1)

        w2sd = sb.tile([P, PACK, P], U8, name="w2sd", tag="yi1", align_bytes=64)
        deal_scales(nc, w2sd, w2s_raw)

        def pieces(h):
            return [slice(0, VH)] if h == 0 else [slice(0, VH // 2), slice(VH // 2, VH)]

        def by_word(ap):
            return ap.rearrange("p (c i) t -> p c t i", i=4)

        def by_row(ap):
            return ap.rearrange("p t (c i) -> p c t i", i=4)

        acc2 = []
        for h in range(2):
            zb = sb.tile([P, VH, PACK], BF16, name="zb%d" % h, tag="slot%d" % h, align_bytes=64)
            zq = sb.tile([P, VH], U32, name="zq%d" % h, align_bytes=64)
            zs = sb.tile([P, VH], U8, name="zs%d" % h, align_bytes=64)
            for c in pieces(h):
                vc = slice(h * VH + c.start, h * VH + c.stop)
                nc.vector.tensor_tensor(out=by_word(zb[:, c, :]), in0=by_row(sq[h][:, :, c]), in1=by_row(gd[:, :, vc]), op=ALU.mult)
            for c in pieces(h):
                nc.vector.quantize_mx(out=zq[:, c].bitcast(FP8X4), scales=zs[:, c], in_=zb[:, c, :].rearrange("p v t -> p (v t)"))
            banks = []
            for u in range(2):
                acc = ps.tile([P, 2, VH], F32, name="out%d%d" % (h, u), tag="acc%d%d" % (u, h))
                for t in range(2 * u, 2 * u + 2):
                    nc.tensor.matmul_mx(
                        out=acc[:, t - 2 * u, :],
                        lhsT=w2d[:, t, :].bitcast(FP4X4),
                        lhsT_scale=w2sd[:, t, :],
                        rhs=zq[:].bitcast(FP8X4),
                        rhs_scale=zs[:],
                        start=True,
                        stop=True,
                    )
                banks.append(acc)
            acc2.append(banks)

        ow = sb.tile([P, V], U32, name="ow", align_bytes=64)
        osc = sb.tile([P, V], U8, name="osc", align_bytes=64)
        out_rows = out_0.rearrange("(p t) v -> p t v", t=PACK)
        out_words = out_1[0].rearrange("p n t -> p (n t)").bitcast(I32)
        for h in range(2):
            vc = slice(h * VH, (h + 1) * VH)
            o = sb.tile([P, PACK, VH], F32, name="o%d" % h, tag="slot%d" % (h + 1), align_bytes=64)
            ob = sb.tile([P, VH, PACK], BF16, name="ob%d" % h, align_bytes=64)
            for u in range(2):
                ts = slice(2 * u, 2 * u + 2)
                nc.vector.tensor_tensor(out=o[:, ts, :], in0=acc2[h][u][:], in1=res_t[:, ts, vc], op=ALU.add)
            for c in pieces(h):
                if c.start == 0:
                    nc.scalar.copy(out=by_word(ob[:, c, :]), in_=by_row(o[:, :, c]))
                else:
                    nc.vector.tensor_copy(out=by_word(ob[:, c, :]), in_=by_row(o[:, :, c]))
            nc.sync.dma_start(out=out_rows[:, :, vc], in_=o[:])
            for c in pieces(h):
                pc = slice(h * VH + c.start, h * VH + c.stop)
                nc.vector.quantize_mx(out=ow[:, pc].bitcast(FP8X4), scales=osc[:, pc], in_=ob[:, c, :].rearrange("p v t -> p (v t)"))
            nc.sync.dma_start(out=out_words[:, vc], in_=ow[:, vc].bitcast(I32))
        for q in range(4):
            queue = nc.scalar if q % 2 == 0 else nc.sync
            queue.dma_start(out=out_2[0, 4 * q : 4 * q + 4, :].bitcast(I32), in_=osc[32 * q : 32 * q + 4, :].bitcast(I32))
